import numpy as np
import ml_dtypes


def mxq(x, axis, fmt="e4m3"):
    dtype, down = {"e4m3": (ml_dtypes.float8_e4m3fn, 7), "e5m2": (ml_dtypes.float8_e5m2, 14)}[fmt]
    v = np.moveaxis(np.asarray(x, np.float32).astype(ml_dtypes.bfloat16).astype(np.float64), axis, -1)
    blocks = v.reshape(v.shape[:-1] + (-1, 32))
    amax = np.abs(blocks).max(-1, keepdims=True)
    byte = np.maximum(np.where(amax > 0, np.frexp(amax)[1] - 1 + 127, 0) - down, 1)
    scale = np.exp2(byte - 127.0)
    codes = (blocks / scale).astype(np.float32).astype(dtype).astype(np.float64)
    return np.moveaxis((codes * scale).reshape(v.shape), -1, axis)


WIDE = False


def mx_kscale(k):
    if not WIDE:
        return np.ones(k)
    levels = np.array([10, -10, 5, -5, 0])
    if k % 512:
        return np.exp2(np.random.permutation(np.resize(levels, k // 32))).repeat(32)
    a = np.empty((k // 512, 16))
    for p in range(k // 512):
        a[p, :8] = np.random.permutation(np.resize(levels, 8))
        for g in range(8):
            far = levels[np.abs(levels - a[p, g]) >= 10]
            a[p, g + 8] = far[np.random.randint(len(far))]
    return np.exp2(a.ravel()).repeat(32)


def f64(x):
    return np.asarray(x).astype(np.float64)


def striped(idx):
    return np.tile(idx.reshape(-1, 16).T, (8, 1)).astype(np.uint16)


def unstriped(offs):
    return offs[:16].T.reshape(-1).astype(np.int64)


E2M1 = np.array([0.0, 0.5, 1.0, 1.5, 2.0, 3.0, 4.0, 6.0, -0.0, -0.5, -1.0, -1.5, -2.0, -3.0, -4.0, -6.0])


def pack_weight(w, fmt):
    k, n = w.shape
    w = f64(np.asarray(w, np.float32).astype(ml_dtypes.bfloat16)).reshape(k // 32, 32, n)
    amax = np.abs(w).max(1)
    if fmt == "e4m3":
        byte = np.frexp(amax)[1] - 1 + 127 - 7
    else:
        mant, ex = np.frexp(amax / 6.0)
        byte = np.where(mant > 0.5, ex, ex - 1) + 127
    byte = np.clip(np.where(amax > 0, byte, 1), 1, 254)
    scaled = (w * np.exp2(127.0 - byte)[:, None, :]).reshape(k, n).astype(np.float32)
    by_word = np.ascontiguousarray(scaled.reshape(k // 512, 128, 4, n).transpose(0, 1, 3, 2))
    if fmt == "e4m3":
        words = by_word.astype(ml_dtypes.float8_e4m3fn).view(np.uint8)
    else:
        c = by_word.astype(ml_dtypes.float4_e2m1fn).view(np.uint8) & 0xF
        words = (c[..., 0::2] | (c[..., 1::2] << 4)).reshape(k // 512, 128, 2 * n)
    return np.ascontiguousarray(words), np.ascontiguousarray(byte.astype(np.uint8).reshape(k // 512, 16, n))


def unpack_weight(words, scales, fmt):
    g, _, n = scales.shape
    words = np.ascontiguousarray(words).reshape(g, 128, n, -1)
    if fmt == "e4m3":
        vals = words.view(ml_dtypes.float8_e4m3fn).astype(np.float64)
    else:
        nib = np.empty((g, 128, n, 4), np.uint8)
        nib[..., 0::2] = words & 0xF
        nib[..., 1::2] = words >> 4
        vals = E2M1[nib]
    vals = vals * np.repeat(np.exp2(scales.astype(np.float64) - 127.0), 8, axis=1)[..., None]
    return vals.transpose(0, 1, 3, 2).reshape(g * 512, n)


def d_silu(v):
    s = 1.0 / (1.0 + np.exp(-np.maximum(v, -700.0)))
    return s * (1.0 + v * (1.0 - s))


K, T, E, C, H, N = 256, 768, 9, 256, 1024, 512
TOP = 3


def by_expert(wq, xq):
    return np.concatenate([wq[e].T @ xq[:, e * C:(e + 1) * C] for e in range(E)], axis=1)


def setup_inputs():
    n = np.random.standard_normal
    s = mx_kscale(N)[:, None]
    u = mx_kscale(H)
    deal = np.repeat(np.arange(E), C).reshape(TOP, T)[:, np.random.permutation(T)]
    deal = np.take_along_axis(deal, np.argsort(np.random.rand(TOP, T), axis=0), axis=0)
    for _ in range(8):
        s_, t_ = np.random.permutation(T).reshape(2, -1); r = np.random.randint(TOP, size=T // 2); x, y = deal[r, s_].copy(), deal[r, t_].copy()
        ok = ~((deal[:, s_] == y).any(0) | (deal[:, t_] == x).any(0)); deal[r[ok], s_[ok]] = y[ok]; deal[r[ok], t_[ok]] = x[ok]
    order = np.lexsort((np.random.rand(TOP * T), deal.reshape(-1)))
    slot_token = order % T; pos = np.empty(TOP * T, np.int64); pos[order] = np.arange(TOP * T); pos = pos.reshape(TOP, T)
    g = np.random.uniform(0.5, 1.5, (TOP, T)); g = g / g.sum(0)
    w_slot = np.empty(E * C)
    for r in range(TOP): w_slot[pos[r]] = g[r]
    w2 = [pack_weight(m, "e2m1") for m in n((E, N, H)) / np.sqrt(N) / s[None] * u[None, None, :]]
    w1 = [pack_weight(m, "e2m1") for m in n((E, H, K)) / np.sqrt(H) / u[None, :, None]]
    return {
        "dyT": (n((N, T)) * s).astype(np.float32),
        "a": n((H, E * C)).astype(np.float32),
        "w2_words": np.stack([m[0] for m in w2]),
        "w2_scales": np.stack([m[1] for m in w2]),
        "w1_words": np.stack([m[0] for m in w1]),
        "w1_scales": np.stack([m[1] for m in w1]),
        "gate": np.tile(w_slot, (N, 1)).astype(np.float32),
        "offs": striped(slot_token),
        "pos1": striped(pos[0]),
        "pos2": striped(pos[1]),
        "pos3": striped(pos[2]),
    }


def reference(dyT, a, w2_words, w2_scales, w1_words, w1_scales, gate, offs, pos1, pos2, pos3):
    idx = unstriped(offs)
    w2 = np.stack([unpack_weight(w2_words[e], w2_scales[e], "e2m1") for e in range(E)])
    w1 = np.stack([unpack_weight(w1_words[e], w1_scales[e], "e2m1") for e in range(E)])
    gq = mxq(f64(gate) * f64(dyT)[:, idx], 0, "e4m3")
    dh = by_expert(w2, gq)
    da = dh * d_silu(f64(a))
    dx = by_expert(w1, mxq(da, 0, "e4m3"))
    return dx[:, unstriped(pos1)] + dx[:, unstriped(pos2)] + dx[:, unstriped(pos3)]

@@ -1,0 +1,343 @@
+from contextlib import ExitStack
+
+import concourse.mybir as mybir
+
+K, T, E, C, H, N = 256, 768, 9, 256, 1024, 512
+S = E * C
+P = 128
+PACK = 4
+PASS = P * PACK
+H_PASSES = H // PASS
+K_BLOCKS = K // P
+LIST_ROWS = 16
+
+FLOPS = 2 * S * (N * H + H * K)
+
+F32 = mybir.dt.float32
+BF16 = mybir.dt.bfloat16
+I32 = mybir.dt.int32
+U32 = mybir.dt.uint32
+U16 = mybir.dt.uint16
+U8 = mybir.dt.uint8
+FP8X4 = mybir.dt.float8_e4m3fn_x4
+FP4X4 = mybir.dt.float4_e2m1fn_x4
+ACT = mybir.ActivationFunctionType
+ALU = mybir.AluOpType
+
+GROUP = 3
+GATE_LOADS = ((0, 1), (1, 5), (5, 9))
+PARKED = {1: 4, 2: 72}
+VECTOR_GATHERS = 1
+SCALAR_PERMUTES = (7, 8)
+
+
+def tile_moe_bdx_mlp_silu_kernel(
+    tc, dyT, a, w2_words, w2_scales, w1_words, w1_scales, gate, offs, pos1, pos2, pos3, out
+):
+    nc = tc.nc
+    with ExitStack() as ctx:
+        keep = ctx.enter_context(tc.tile_pool(name="keep", bufs=1))
+        ring = ctx.enter_context(tc.tile_pool(name="ring", bufs=2))
+        psum = ctx.enter_context(tc.psum_pool(name="psum", bufs=1))
+
+        offs_sb = keep.tile([P, S // LIST_ROWS], U16, name="offs_sb")
+        pos_sb = [keep.tile([P, T // LIST_ROWS], U16, name=f"pos_sb{r}") for r in range(3)]
+        dy_sb = [keep.tile([P, T], F32, name=f"dy_sb{t}") for t in range(PACK)]
+        gate_sb = [keep.tile([P, (hi - lo) * C], F32, name=f"gate_sb{lo}") for lo, hi in GATE_LOADS]
+        w1_sb = [
+            keep.tile([P, GROUP * H_PASSES, 2 * K], U8, name=f"w1_sb{g}", align_bytes=64)
+            for g in range(E // GROUP)
+        ]
+        s2_raw = keep.tile([P, GROUP, H], U8, name="s2_raw", align_bytes=64)
+        s2_sb = [keep.tile([P, GROUP, H], U8, name=f"s2_sb{g}", align_bytes=64) for g in range(E // GROUP)]
+        s1_sb = keep.tile([P, E * H_PASSES, K], U8, name="s1_sb", align_bytes=64)
+        dx_sb = [keep.tile([P, S], F32, name=f"dx_sb{b}") for b in range(K_BLOCKS)]
+
+        nc.vector.memset(s2_raw[:].rearrange("p e i -> p (e i)").bitcast(I32), 0)
+        for plane in s2_sb[1:] + [s1_sb]:
+            nc.gpsimd.memset(plane[:].rearrange("p e k -> p (e k)").bitcast(I32), 0)
+
+        a_sb, w2_raw, w2_perm = {}, {}, {}
+        g_f32, g_bf, g_codes, g_scales = {}, {}, {}, {}
+        neg_tanh, silu_neg, banks, x_sb = {}, {}, {}, {}
+        da_bf, da_codes, da_scales, dx_bank = {}, {}, {}, {}
+
+        dy_rows = dyT.rearrange("(p t) c -> t p c", t=PACK)
+        a_rows = a.rearrange("(h p t) j -> h p t j", h=H_PASSES, t=PACK)
+
+        def load_a(e, passes=range(H_PASSES)):
+            for h in passes:
+                a_sb[e, h] = ring.tile([P, PACK, C], F32, name="a_sb", bufs=8)
+                nc.sync.dma_start(a_sb[e, h][:], a_rows[h][:, :, e * C : (e + 1) * C])
+
+        def load_w2(e):
+            w2_raw[e] = ring.tile([P, 2 * H], U8, name="w2_raw", bufs=4, align_bytes=64)
+            nc.sync.dma_start(w2_raw[e][:].bitcast(I32), w2_words[e, 0].bitcast(I32))
+
+        def load_gate(g):
+            lo, hi = GATE_LOADS[g]
+            nc.sync.dma_start(gate_sb[g][:], gate[0:P, lo * C : hi * C])
+
+        def gates_of(e):
+            g = [lo <= e < hi for lo, hi in GATE_LOADS].index(True)
+            first = (e - GATE_LOADS[g][0]) * C
+            return gate_sb[g][:, first : first + C]
+
+        def load_w1(g):
+            src = w1_words[g * GROUP : (g + 1) * GROUP].rearrange("e s p b -> p (e s) b")
+            nc.sync.dma_start(w1_sb[g][:].bitcast(I32), src.bitcast(I32))
+
+        def load_s2():
+            src = w2_scales[0:GROUP].rearrange("e s (q r) i -> r q (e s) i", r=4)
+            for r in range(4):
+                nc.sync.dma_start(s2_raw[r:P:32].bitcast(I32), src[r].bitcast(I32))
+            for g, first in PARKED.items():
+                rows = w2_scales[g * GROUP : (g + 1) * GROUP].rearrange("e s f i -> f (e s) i")
+                nc.sync.dma_start(s2_raw[first : first + 16].bitcast(I32), rows.bitcast(I32))
+
+        def move_s2(g):
+            for q in range(4):
+                first = PARKED[g] + 4 * q
+                nc.sync.dma_start(
+                    s2_sb[g][32 * q : 32 * q + 4].bitcast(I32), s2_sb[0][first : first + 4].bitcast(I32)
+                )
+
+        def load_s1():
+            src = w1_scales.rearrange("e s (q r) k -> r q (e s) k", r=4)
+            for r in range(4):
+                nc.sync.dma_start(s1_sb[r:P:32].bitcast(I32), src[r].bitcast(I32))
+
+        def permute_w2(e):
+            w2_perm[e] = ring.tile([P, 2 * H], U8, name="w2_perm", bufs=3, align_bytes=64)
+            copy = nc.scalar.copy if e in SCALAR_PERMUTES else nc.vector.tensor_copy
+            copy(
+                w2_perm[e][:].bitcast(U16).rearrange("p (h t m) -> p h t m", h=H_PASSES, t=PACK),
+                w2_raw[e][:].bitcast(U16).rearrange("p (h m t) -> p h t m", h=H_PASSES, t=PACK),
+            )
+
+        def permute_s2(lo, hi):
+            nc.vector.tensor_copy(
+                s2_sb[0][:, lo:hi, :].rearrange("p e (h t m) -> p (e h) t m", h=H_PASSES, t=PACK),
+                s2_raw[:, lo:hi, :].rearrange("p e (h m t) -> p (e h) t m", h=H_PASSES, t=PACK),
+            )
+
+        def gather_g(e):
+            g_f32[e] = ring.tile([P, PACK, C], F32, name="g_f32", bufs=3)
+            cols = slice(e * C // LIST_ROWS, (e + 1) * C // LIST_ROWS)
+            for t in range(PACK):
+                window = dy_sb[t][:].indirect(offs_sb[:, cols])
+                if e < VECTOR_GATHERS:
+                    nc.vector.tensor_tensor(g_f32[e][:, t, :], window, gates_of(e), ALU.mult)
+                else:
+                    nc.scalar.activation(g_f32[e][:, t, :], window, ACT.Copy)
+
+        def gate_g(e):
+            g_bf[e] = ring.tile([P, C * PACK], BF16, name="g_bf", bufs=2, align_bytes=64)
+            dst = g_bf[e][:].rearrange("p (c i t) -> p c t i", i=4, t=PACK)
+            src = g_f32[e][:].rearrange("p t (c i) -> p c t i", i=4)
+            if e < VECTOR_GATHERS:
+                nc.vector.tensor_copy(dst, src)
+            else:
+                gates = gates_of(e).rearrange("p (c i) -> p c i", i=4).unsqueeze(2)
+                nc.vector.tensor_tensor(dst, src, gates.to_broadcast([P, C // 4, PACK, 4]), ALU.mult)
+
+        def quantize_g(e):
+            g_codes[e] = ring.tile([P, C], U32, name="g_codes", bufs=3, align_bytes=64)
+            g_scales[e] = ring.tile([P, C], U8, name="g_scales", bufs=3, align_bytes=64)
+            nc.vector.quantize_mx(out=g_codes[e][:].bitcast(FP8X4), scales=g_scales[e][:], in_=g_bf[e][:])
+
+        def activations(e, h):
+            neg_tanh[e, h] = ring.tile([P, 2, C, 2], F32, name="neg_tanh", bufs=4)
+            silu_neg[e, h] = ring.tile([P, 2, C, 2], F32, name="silu_neg", bufs=4)
+            src = a_sb[e, h][:].rearrange("p (u v) s -> p v s u", u=2)
+            nc.scalar.activation(silu_neg[e, h][:], src, ACT.Silu, scale=-1.0)
+            nc.scalar.activation(neg_tanh[e, h][:], src, ACT.Tanh, scale=-0.5)
+
+        def matmul_w2(e, h):
+            for v in range(2):
+                slot = ((e * H_PASSES + h) * 2 + v) % 6
+                banks[e, h, v] = psum.tile([P, 2, C], F32, name=f"dh_bank{slot}")
+                for u in range(2):
+                    col = (h * PACK + 2 * u + v) * P
+                    nc.tensor.matmul_mx(
+                        out=banks[e, h, v][:, u, :],
+                        lhsT=w2_perm[e][:, 2 * col : 2 * (col + P)].bitcast(FP4X4),
+                        lhsT_scale=s2_sb[e // GROUP][:, e % GROUP, col : col + P],
+                        rhs=g_codes[e][:].bitcast(FP8X4),
+                        rhs_scale=g_scales[e][:],
+                        start=True,
+                        stop=True,
+                    )
+
+        def times_sigmoid(e, h, v):
+            if v == 0:
+                x_sb[e, h] = ring.tile([P, 2, C, 2], F32, name="x_sb", bufs=3)
+            nc.vector.scalar_tensor_tensor(
+                x_sb[e, h][:, v],
+                neg_tanh[e, h][:, v],
+                1.0,
+                banks[e, h, v][:].rearrange("p u s -> p s u"),
+                ALU.subtract,
+                ALU.mult,
+            )
+
+        def finish_da(e, h):
+            if h == 0:
+                da_bf[e] = ring.tile([P, H_PASSES, C * PACK], BF16, name="da_bf", bufs=2, align_bytes=64)
+            nc.vector.scalar_tensor_tensor(
+                da_bf[e][:, h, :].rearrange("p (y v) -> p y v", v=2),
+                silu_neg[e, h][:].rearrange("p v s u -> p (s u) v"),
+                1.0,
+                x_sb[e, h][:].rearrange("p v s u -> p (s u) v"),
+                ALU.subtract,
+                ALU.mult,
+            )
+
+        def quantize_da(e, lo, hi):
+            if lo == 0:
+                da_codes[e] = ring.tile([P, H_PASSES * C], U32, name="da_codes", bufs=2, align_bytes=64)
+                da_scales[e] = ring.tile([P, H_PASSES * C], U8, name="da_scales", bufs=2, align_bytes=64)
+            nc.vector.quantize_mx(
+                out=da_codes[e][:, lo * C : hi * C].bitcast(FP8X4),
+                scales=da_scales[e][:, lo * C : hi * C],
+                in_=da_bf[e][:, lo:hi, :].rearrange("p h x -> p (h x)"),
+            )
+
+        def matmul_w1(e):
+            if e % 2 == 0:
+                for b in range(K_BLOCKS):
+                    dx_bank[b] = psum.tile([P, 2 * C], F32, name=f"dx_bank{b}")
+            for h in range(H_PASSES):
+                for b in range(K_BLOCKS):
+                    row = (e % GROUP) * H_PASSES + h
+                    nc.tensor.matmul_mx(
+                        out=dx_bank[b][:, (e % 2) * C : (e % 2 + 1) * C],
+                        lhsT=w1_sb[e // GROUP][:, row, 2 * b * P : 2 * (b + 1) * P].bitcast(FP4X4),
+                        lhsT_scale=s1_sb[:, e * H_PASSES + h, b * P : (b + 1) * P],
+                        rhs=da_codes[e][:, h * C : (h + 1) * C].bitcast(FP8X4),
+                        rhs_scale=da_scales[e][:, h * C : (h + 1) * C],
+                        start=(h == 0),
+                        stop=(h == H_PASSES - 1),
+                    )
+
+        def store_dx(e):
+            if e % 2 == 1:
+                for b in range(K_BLOCKS):
+                    nc.scalar.activation(dx_sb[b][:, (e - 1) * C : (e + 1) * C], dx_bank[b][:], ACT.Copy, scale=0.5)
+            elif e == E - 1:
+                nc.scalar.activation(dx_sb[1][:, e * C :], dx_bank[1][:, 0:C], ACT.Copy, scale=0.5)
+                nc.vector.tensor_scalar_mul(dx_sb[0][:, e * C :], dx_bank[0][:, 0:C], 0.5)
+
+        nc.sync.dma_start(offs_sb[:], offs)
+        load_a(0, [0])
+        load_w2(0)
+        load_gate(0)
+        nc.sync.dma_start(dy_sb[0][:], dy_rows[0])
+        nc.sync.dma_start(dy_sb[1][:], dy_rows[1])
+        nc.sync.dma_start(dy_sb[2][:], dy_rows[2])
+        nc.sync.dma_start(dy_sb[3][:], dy_rows[3])
+        load_s2()
+        load_a(0, [1])
+        load_gate(1)
+        load_w2(1)
+        load_a(1)
+        load_s1()
+        load_w1(0)
+        load_w2(2)
+        load_a(2)
+        load_w1(1)
+        load_gate(2)
+        load_a(3)
+        load_w1(2)
+        for lst, src in zip(pos_sb, (pos1, pos2, pos3)):
+            nc.sync.dma_start(lst[:], src)
+
+        activations(0, 0)
+        gather_g(0)
+        gate_g(0)
+        permute_w2(0)
+        quantize_g(0)
+        permute_s2(0, 1)
+        gather_g(1)
+        activations(0, 1)
+        permute_w2(1)
+        permute_s2(1, GROUP)
+        gate_g(1)
+        move_s2(1)
+        move_s2(2)
+        quantize_g(1)
+        for e in range(E):
+            if e + 3 < E:
+                load_w2(e + 3)
+            if e + 4 < E:
+                load_a(e + 4)
+            matmul_w2(e, 0)
+            matmul_w2(e, 1)
+            if e + 1 < E:
+                activations(e + 1, 0)
+            times_sigmoid(e, 0, 0)
+            times_sigmoid(e, 0, 1)
+            times_sigmoid(e, 1, 0)
+            finish_da(e, 0)
+            if e > 0:
+                matmul_w1(e - 1)
+                store_dx(e - 1)
+            times_sigmoid(e, 1, 1)
+            if e == E - 1:
+                quantize_da(e, 0, 1)
+            if e + 1 < E:
+                activations(e + 1, 1)
+            if e + 2 < E:
+                gather_g(e + 2)
+                permute_w2(e + 2)
+            finish_da(e, 1)
+            if e + 2 < E:
+                gate_g(e + 2)
+            quantize_da(e, 1 if e == E - 1 else 0, H_PASSES)
+            if e + 2 < E:
+                quantize_g(e + 2)
+        matmul_w1(E - 1)
+        store_dx(E - 1)
+
+        half = T // 2
+
+        def window(b, c, r):
+            return dx_sb[b][:].indirect(pos_sb[r][:, c * half // LIST_ROWS : (c + 1) * half // LIST_ROWS])
+
+        def part(name):
+            return keep.tile([P, half], F32, name=name)
+
+        def on_scalar(b, c, r):
+            picked = part(f"picked{b}{c}{r}")
+            nc.scalar.activation(picked[:], window(b, c, r), ACT.Copy)
+            return picked
+
+        def gather_add(b, c, r, other):
+            total = part(f"sum{b}{c}{r}")
+            nc.vector.tensor_tensor(total[:], window(b, c, r), other[:], ALU.add)
+            return total
+
+        def plain_add(b, c, x, y):
+            total = part(f"total{b}{c}")
+            nc.vector.tensor_tensor(total[:], x[:], y[:], ALU.add)
+            return total
+
+        def store(b, c, total):
+            nc.sync.dma_start(out[b * P : (b + 1) * P, c * half : (c + 1) * half], total[:])
+
+        a10 = on_scalar(1, 0, 0)
+        a00 = on_scalar(0, 0, 0)
+        a01 = on_scalar(0, 1, 0)
+        a11 = on_scalar(1, 1, 0)
+        b01 = on_scalar(0, 1, 1)
+        b11 = on_scalar(1, 1, 1)
+        v00 = part("first00")
+        nc.vector.tensor_copy(v00[:], window(0, 0, 1))
+        v10 = gather_add(1, 0, 1, a10)
+        v00 = gather_add(0, 0, 2, v00)
+        store(1, 0, gather_add(1, 0, 2, v10))
+        store(0, 0, plain_add(0, 0, v00, a00))
+        v01 = gather_add(0, 1, 2, a01)
+        v11 = gather_add(1, 1, 2, a11)
+        store(0, 1, plain_add(0, 1, v01, b01))
+        store(1, 1, plain_add(1, 1, v11, b11))

@@ -25,7 +25,8 @@ ACT = mybir.ActivationFunctionType
 ALU = mybir.AluOpType
 
 GROUP = 3
-GATE_LOADS = ((0, 1), (1, 5), (5, 9))
+GATE_LOADS = ((0, 1), (1, 3), (3, 6), (6, 9))
+TOKEN_CUTS = (0, 160, 768)
 PARKED = {1: 4, 2: 72}
 VECTOR_GATHERS = 1
 SCALAR_PERMUTES = (7, 8)
@@ -54,8 +55,9 @@ def tile_moe_bdx_mlp_silu_kernel(
         dx_sb = [keep.tile([P, S], F32, name=f"dx_sb{b}") for b in range(K_BLOCKS)]
 
         nc.vector.memset(s2_raw[:].rearrange("p e i -> p (e i)").bitcast(I32), 0)
-        for plane in s2_sb[1:] + [s1_sb]:
-            nc.gpsimd.memset(plane[:].rearrange("p e k -> p (e k)").bitcast(I32), 0)
+        nc.gpsimd.memset(s1_sb[:].rearrange("p e k -> p (e k)").bitcast(I32), 0)
+        for plane in s2_sb[1:]:
+            nc.vector.memset(plane[:].rearrange("p e k -> p (e k)").bitcast(I32), 0)
 
         a_sb, w2_raw, w2_perm = {}, {}, {}
         g_f32, g_bf, g_codes, g_scales = {}, {}, {}, {}
@@ -102,10 +104,10 @@ def tile_moe_bdx_mlp_silu_kernel(
                     s2_sb[g][32 * q : 32 * q + 4].bitcast(I32), s2_sb[0][first : first + 4].bitcast(I32)
                 )
 
-        def load_s1():
-            src = w1_scales.rearrange("e s (q r) k -> r q (e s) k", r=4)
+        def load_s1(lo=0, hi=E):
+            src = w1_scales[lo:hi].rearrange("e s (q r) k -> r q (e s) k", r=4)
             for r in range(4):
-                nc.sync.dma_start(s1_sb[r:P:32].bitcast(I32), src[r].bitcast(I32))
+                nc.gpsimd.dma_start(s1_sb[r:P:32, lo * H_PASSES : hi * H_PASSES].bitcast(I32), src[r].bitcast(I32))
 
         def permute_w2(e):
             w2_perm[e] = ring.tile([P, 2 * H], U8, name="w2_perm", bufs=3, align_bytes=64)
@@ -133,13 +135,13 @@ def tile_moe_bdx_mlp_silu_kernel(
 
         def gate_g(e):
             g_bf[e] = ring.tile([P, C * PACK], BF16, name="g_bf", bufs=2, align_bytes=64)
-            dst = g_bf[e][:].rearrange("p (c i t) -> p c t i", i=4, t=PACK)
-            src = g_f32[e][:].rearrange("p t (c i) -> p c t i", i=4)
+            dst = g_bf[e][:].rearrange("p (c i t) -> p c t i", i=2, t=PACK)
+            src = g_f32[e][:].rearrange("p t (c i) -> p c t i", i=2)
             if e < VECTOR_GATHERS:
                 nc.vector.tensor_copy(dst, src)
             else:
-                gates = gates_of(e).rearrange("p (c i) -> p c i", i=4).unsqueeze(2)
-                nc.vector.tensor_tensor(dst, src, gates.to_broadcast([P, C // 4, PACK, 4]), ALU.mult)
+                gates = gates_of(e).rearrange("p (c i) -> p c i", i=2).unsqueeze(2)
+                nc.vector.tensor_tensor(dst, src, gates.to_broadcast([P, C // 2, PACK, 2]), ALU.mult)
 
         def quantize_g(e):
             g_codes[e] = ring.tile([P, C], U32, name="g_codes", bufs=3, align_bytes=64)
@@ -228,6 +230,7 @@ def tile_moe_bdx_mlp_silu_kernel(
                 nc.scalar.activation(dx_sb[1][:, e * C :], dx_bank[1][:, 0:C], ACT.Copy, scale=0.5)
                 nc.vector.tensor_scalar_mul(dx_sb[0][:, e * C :], dx_bank[0][:, 0:C], 0.5)
 
+        load_s1()
         nc.sync.dma_start(offs_sb[:], offs)
         load_a(0, [0])
         load_w2(0)
@@ -241,16 +244,9 @@ def tile_moe_bdx_mlp_silu_kernel(
         load_gate(1)
         load_w2(1)
         load_a(1)
-        load_s1()
-        load_w1(0)
         load_w2(2)
+        load_w1(0)
         load_a(2)
-        load_w1(1)
-        load_gate(2)
-        load_a(3)
-        load_w1(2)
-        for lst, src in zip(pos_sb, (pos1, pos2, pos3)):
-            nc.sync.dma_start(lst[:], src)
 
         activations(0, 0)
         gather_g(0)
@@ -263,14 +259,34 @@ def tile_moe_bdx_mlp_silu_kernel(
         permute_w2(1)
         permute_s2(1, GROUP)
         gate_g(1)
-        move_s2(1)
-        move_s2(2)
         quantize_g(1)
         for e in range(E):
-            if e + 3 < E:
-                load_w2(e + 3)
-            if e + 4 < E:
-                load_a(e + 4)
+            if e == 0:
+                load_gate(2)
+                load_w2(3)
+                load_a(3)
+                move_s2(1)
+            if e == 1:
+                load_w2(4)
+                load_a(4)
+                load_w1(1)
+            if e == 2:
+                load_w2(5)
+                load_gate(3)
+                load_a(5)
+            if e == 3:
+                load_w2(6)
+                load_a(6)
+                move_s2(2)
+            if e == 4:
+                load_w2(7)
+                load_a(7)
+                load_w1(2)
+            if e == 5:
+                load_w2(8)
+                load_a(8)
+            if e == 6:
+                for lst, src in zip(pos_sb, (pos1, pos2, pos3)): nc.sync.dma_start(lst[:], src)
             matmul_w2(e, 0)
             matmul_w2(e, 1)
             if e + 1 < E:
@@ -299,45 +315,47 @@ def tile_moe_bdx_mlp_silu_kernel(
         matmul_w1(E - 1)
         store_dx(E - 1)
 
-        half = T // 2
-
         def window(b, c, r):
-            return dx_sb[b][:].indirect(pos_sb[r][:, c * half // LIST_ROWS : (c + 1) * half // LIST_ROWS])
+            lo, hi = TOKEN_CUTS[c], TOKEN_CUTS[c + 1]
+            return dx_sb[b][:].indirect(pos_sb[r][:, lo // LIST_ROWS : hi // LIST_ROWS])
 
-        def part(name):
-            return keep.tile([P, half], F32, name=name)
+        def part(name, c):
+            return keep.tile([P, TOKEN_CUTS[c + 1] - TOKEN_CUTS[c]], F32, name=name)
 
         def on_scalar(b, c, r):
-            picked = part(f"picked{b}{c}{r}")
+            picked = part(f"picked{b}{c}{r}", c)
             nc.scalar.activation(picked[:], window(b, c, r), ACT.Copy)
             return picked
 
+        def on_vector(b, c, r):
+            picked = part(f"picked{b}{c}{r}", c)
+            nc.vector.tensor_copy(picked[:], window(b, c, r))
+            return picked
+
         def gather_add(b, c, r, other):
-            total = part(f"sum{b}{c}{r}")
+            total = part(f"sum{b}{c}{r}", c)
             nc.vector.tensor_tensor(total[:], window(b, c, r), other[:], ALU.add)
             return total
 
         def plain_add(b, c, x, y):
-            total = part(f"total{b}{c}")
+            total = part(f"total{b}{c}", c)
             nc.vector.tensor_tensor(total[:], x[:], y[:], ALU.add)
             return total
 
         def store(b, c, total):
-            nc.sync.dma_start(out[b * P : (b + 1) * P, c * half : (c + 1) * half], total[:])
+            nc.sync.dma_start(out[b * P : (b + 1) * P, TOKEN_CUTS[c] : TOKEN_CUTS[c + 1]], total[:])
 
-        a10 = on_scalar(1, 0, 0)
-        a00 = on_scalar(0, 0, 0)
-        a01 = on_scalar(0, 1, 0)
         a11 = on_scalar(1, 1, 0)
-        b01 = on_scalar(0, 1, 1)
+        a01 = on_scalar(0, 1, 0)
         b11 = on_scalar(1, 1, 1)
-        v00 = part("first00")
-        nc.vector.tensor_copy(v00[:], window(0, 0, 1))
-        v10 = gather_add(1, 0, 1, a10)
-        v00 = gather_add(0, 0, 2, v00)
+        b01 = on_scalar(0, 1, 1)
+        v00 = on_vector(0, 0, 0)
+        v10 = on_vector(1, 0, 0)
+        v00 = gather_add(0, 0, 1, v00)
+        v10 = gather_add(1, 0, 1, v10)
+        store(0, 0, gather_add(0, 0, 2, v00))
         store(1, 0, gather_add(1, 0, 2, v10))
-        store(0, 0, plain_add(0, 0, v00, a00))
-        v01 = gather_add(0, 1, 2, a01)
         v11 = gather_add(1, 1, 2, a11)
-        store(0, 1, plain_add(0, 1, v01, b01))
+        v01 = gather_add(0, 1, 2, a01)
         store(1, 1, plain_add(1, 1, v11, b11))
+        store(0, 1, plain_add(0, 1, v01, b01))

@@ -6,10 +6,12 @@ K, T, E, C, H, N = 256, 768, 9, 256, 1024, 512
 S = E * C
 P = 128
 PACK = 4
-PASS = P * PACK
-H_PASSES = H // PASS
+H_PASSES = H // (P * PACK)
 K_BLOCKS = K // P
 LIST_ROWS = 16
+SCALE_ROWS = 16
+QUADRANT = 32
+TRIO = 3
 
 FLOPS = 2 * S * (N * H + H * K)
 
@@ -24,12 +26,14 @@ FP4X4 = mybir.dt.float4_e2m1fn_x4
 ACT = mybir.ActivationFunctionType
 ALU = mybir.AluOpType
 
-GROUP = 3
-GATE_LOADS = ((0, 1), (1, 3), (3, 6), (6, 9))
-TOKEN_CUTS = (0, 160, 768)
+GATE_LOADS = ((0, 1), (1, TRIO), (TRIO, 2 * TRIO), (2 * TRIO, E))
 PARKED = {1: 4, 2: 72}
-VECTOR_GATHERS = 1
-SCALAR_PERMUTES = (7, 8)
+DH_BANKS = 6
+LOAD_AHEAD = 3
+
+GPSIMD_SLOTS = 160
+VECTOR_DX_EXPERTS = 4
+VECTOR_TOKENS = 160
 
 
 def tile_moe_bdx_mlp_silu_kernel(
@@ -46,72 +50,67 @@ def tile_moe_bdx_mlp_silu_kernel(
         dy_sb = [keep.tile([P, T], F32, name=f"dy_sb{t}") for t in range(PACK)]
         gate_sb = [keep.tile([P, (hi - lo) * C], F32, name=f"gate_sb{lo}") for lo, hi in GATE_LOADS]
         w1_sb = [
-            keep.tile([P, GROUP * H_PASSES, 2 * K], U8, name=f"w1_sb{g}", align_bytes=64)
-            for g in range(E // GROUP)
+            keep.tile([P, TRIO * H_PASSES, 2 * K], U8, name=f"w1_sb{j}", align_bytes=64) for j in range(E // TRIO)
         ]
-        s2_raw = keep.tile([P, GROUP, H], U8, name="s2_raw", align_bytes=64)
-        s2_sb = [keep.tile([P, GROUP, H], U8, name=f"s2_sb{g}", align_bytes=64) for g in range(E // GROUP)]
         s1_sb = keep.tile([P, E * H_PASSES, K], U8, name="s1_sb", align_bytes=64)
+        s2_raw = keep.tile([P, TRIO, H], U8, name="s2_raw", align_bytes=64)
+        s2_sb = [keep.tile([P, TRIO, H], U8, name=f"s2_sb{j}", align_bytes=64) for j in range(E // TRIO)]
         dx_sb = [keep.tile([P, S], F32, name=f"dx_sb{b}") for b in range(K_BLOCKS)]
 
         nc.vector.memset(s2_raw[:].rearrange("p e i -> p (e i)").bitcast(I32), 0)
         nc.gpsimd.memset(s1_sb[:].rearrange("p e k -> p (e k)").bitcast(I32), 0)
         for plane in s2_sb[1:]:
-            nc.vector.memset(plane[:].rearrange("p e k -> p (e k)").bitcast(I32), 0)
+            nc.vector.memset(plane[:].rearrange("p e i -> p (e i)").bitcast(I32), 0)
 
         a_sb, w2_raw, w2_perm = {}, {}, {}
         g_f32, g_bf, g_codes, g_scales = {}, {}, {}, {}
-        neg_tanh, silu_neg, banks, x_sb = {}, {}, {}, {}
+        tanh_sb, silu_sb, dh_bank, half_da = {}, {}, {}, {}
         da_bf, da_codes, da_scales, dx_bank = {}, {}, {}, {}
 
         dy_rows = dyT.rearrange("(p t) c -> t p c", t=PACK)
         a_rows = a.rearrange("(h p t) j -> h p t j", h=H_PASSES, t=PACK)
 
-        def load_a(e, passes=range(H_PASSES)):
-            for h in passes:
-                a_sb[e, h] = ring.tile([P, PACK, C], F32, name="a_sb", bufs=8)
-                nc.sync.dma_start(a_sb[e, h][:], a_rows[h][:, :, e * C : (e + 1) * C])
+
+        def load_a(e, h):
+            a_sb[e, h] = ring.tile([P, PACK, C], F32, name="a_sb", bufs=8)
+            nc.sync.dma_start(a_sb[e, h][:], a_rows[h][:, :, e * C : (e + 1) * C])
 
         def load_w2(e):
             w2_raw[e] = ring.tile([P, 2 * H], U8, name="w2_raw", bufs=4, align_bytes=64)
             nc.sync.dma_start(w2_raw[e][:].bitcast(I32), w2_words[e, 0].bitcast(I32))
 
-        def load_gate(g):
-            lo, hi = GATE_LOADS[g]
-            nc.sync.dma_start(gate_sb[g][:], gate[0:P, lo * C : hi * C])
+        def load_gate(j):
+            lo, hi = GATE_LOADS[j]
+            nc.sync.dma_start(gate_sb[j][:], gate[0:P, lo * C : hi * C])
 
-        def gates_of(e):
-            g = [lo <= e < hi for lo, hi in GATE_LOADS].index(True)
-            first = (e - GATE_LOADS[g][0]) * C
-            return gate_sb[g][:, first : first + C]
+        def load_w1(j):
+            src = w1_words[j * TRIO : (j + 1) * TRIO].rearrange("e s p b -> p (e s) b")
+            nc.sync.dma_start(w1_sb[j][:].bitcast(I32), src.bitcast(I32))
 
-        def load_w1(g):
-            src = w1_words[g * GROUP : (g + 1) * GROUP].rearrange("e s p b -> p (e s) b")
-            nc.sync.dma_start(w1_sb[g][:].bitcast(I32), src.bitcast(I32))
+        def load_s1():
+            src = w1_scales.rearrange("e s (q r) k -> r q (e s) k", r=4)
+            for r in range(4):
+                nc.gpsimd.dma_start(s1_sb[r:P:QUADRANT].bitcast(I32), src[r].bitcast(I32))
 
         def load_s2():
-            src = w2_scales[0:GROUP].rearrange("e s (q r) i -> r q (e s) i", r=4)
+            src = w2_scales[0:TRIO].rearrange("e s (q r) i -> r q (e s) i", r=4)
             for r in range(4):
-                nc.sync.dma_start(s2_raw[r:P:32].bitcast(I32), src[r].bitcast(I32))
-            for g, first in PARKED.items():
-                rows = w2_scales[g * GROUP : (g + 1) * GROUP].rearrange("e s f i -> f (e s) i")
-                nc.sync.dma_start(s2_raw[first : first + 16].bitcast(I32), rows.bitcast(I32))
+                nc.sync.dma_start(s2_raw[r:P:QUADRANT].bitcast(I32), src[r].bitcast(I32))
+            for j, first in PARKED.items():
+                rows = w2_scales[j * TRIO : (j + 1) * TRIO].rearrange("e s f i -> f (e s) i")
+                nc.sync.dma_start(s2_raw[first : first + SCALE_ROWS].bitcast(I32), rows.bitcast(I32))
 
-        def move_s2(g):
+        def move_s2(j):
             for q in range(4):
-                first = PARKED[g] + 4 * q
+                first = PARKED[j] + 4 * q
                 nc.sync.dma_start(
-                    s2_sb[g][32 * q : 32 * q + 4].bitcast(I32), s2_sb[0][first : first + 4].bitcast(I32)
+                    s2_sb[j][QUADRANT * q : QUADRANT * q + 4].bitcast(I32), s2_sb[0][first : first + 4].bitcast(I32)
                 )
 
-        def load_s1(lo=0, hi=E):
-            src = w1_scales[lo:hi].rearrange("e s (q r) k -> r q (e s) k", r=4)
-            for r in range(4):
-                nc.gpsimd.dma_start(s1_sb[r:P:32, lo * H_PASSES : hi * H_PASSES].bitcast(I32), src[r].bitcast(I32))
 
         def permute_w2(e):
+            copy = nc.scalar.copy if e == E - 1 else nc.vector.tensor_copy
             w2_perm[e] = ring.tile([P, 2 * H], U8, name="w2_perm", bufs=3, align_bytes=64)
-            copy = nc.scalar.copy if e in SCALAR_PERMUTES else nc.vector.tensor_copy
             copy(
                 w2_perm[e][:].bitcast(U16).rearrange("p (h t m) -> p h t m", h=H_PASSES, t=PACK),
                 w2_raw[e][:].bitcast(U16).rearrange("p (h m t) -> p h t m", h=H_PASSES, t=PACK),
@@ -123,74 +122,91 @@ def tile_moe_bdx_mlp_silu_kernel(
                 s2_raw[:, lo:hi, :].rearrange("p e (h m t) -> p (e h) t m", h=H_PASSES, t=PACK),
             )
 
+
+        def gates_of(e):
+            j = [lo <= e < hi for lo, hi in GATE_LOADS].index(True)
+            first = (e - GATE_LOADS[j][0]) * C
+            return gate_sb[j][:, first : first + C]
+
         def gather_g(e):
             g_f32[e] = ring.tile([P, PACK, C], F32, name="g_f32", bufs=3)
             cols = slice(e * C // LIST_ROWS, (e + 1) * C // LIST_ROWS)
             for t in range(PACK):
                 window = dy_sb[t][:].indirect(offs_sb[:, cols])
-                if e < VECTOR_GATHERS:
+                if e == 0:
                     nc.vector.tensor_tensor(g_f32[e][:, t, :], window, gates_of(e), ALU.mult)
                 else:
                     nc.scalar.activation(g_f32[e][:, t, :], window, ACT.Copy)
 
-        def gate_g(e):
-            g_bf[e] = ring.tile([P, C * PACK], BF16, name="g_bf", bufs=2, align_bytes=64)
-            dst = g_bf[e][:].rearrange("p (c i t) -> p c t i", i=2, t=PACK)
-            src = g_f32[e][:].rearrange("p t (c i) -> p c t i", i=2)
-            if e < VECTOR_GATHERS:
+        def new_g_bf(e):
+            g_bf[e] = ring.tile([P, C * PACK], BF16, name="g_bf", bufs=1, align_bytes=64)
+
+        def gate_on_gpsimd(e):
+            nc.gpsimd.tensor_tensor(
+                g_bf[e][:, : GPSIMD_SLOTS * PACK].rearrange("p (s t) -> p s t", t=PACK),
+                g_f32[e][:, :, :GPSIMD_SLOTS].rearrange("p t s -> p s t"),
+                gates_of(e)[:, :GPSIMD_SLOTS].unsqueeze(2).to_broadcast([P, GPSIMD_SLOTS, PACK]),
+                ALU.mult,
+            )
+
+        def gate_on_vector(e, first):
+            dst = g_bf[e][:, first * PACK :].rearrange("p (c i t) -> p c t i", i=2, t=PACK)
+            src = g_f32[e][:, :, first:].rearrange("p t (c i) -> p c t i", i=2)
+            if e == 0:
                 nc.vector.tensor_copy(dst, src)
             else:
-                gates = gates_of(e).rearrange("p (c i) -> p c i", i=2).unsqueeze(2)
-                nc.vector.tensor_tensor(dst, src, gates.to_broadcast([P, C // 2, PACK, 2]), ALU.mult)
+                gates = gates_of(e)[:, first:].rearrange("p (c i) -> p c i", i=2).unsqueeze(2)
+                nc.vector.tensor_tensor(dst, src, gates.to_broadcast([P, (C - first) // 2, PACK, 2]), ALU.mult)
 
         def quantize_g(e):
             g_codes[e] = ring.tile([P, C], U32, name="g_codes", bufs=3, align_bytes=64)
             g_scales[e] = ring.tile([P, C], U8, name="g_scales", bufs=3, align_bytes=64)
             nc.vector.quantize_mx(out=g_codes[e][:].bitcast(FP8X4), scales=g_scales[e][:], in_=g_bf[e][:])
 
+
         def activations(e, h):
-            neg_tanh[e, h] = ring.tile([P, 2, C, 2], F32, name="neg_tanh", bufs=4)
-            silu_neg[e, h] = ring.tile([P, 2, C, 2], F32, name="silu_neg", bufs=4)
+            tanh_sb[e, h] = ring.tile([P, 2, C, 2], F32, name="tanh_sb", bufs=4)
+            silu_sb[e, h] = ring.tile([P, 2, C, 2], F32, name="silu_sb", bufs=4)
             src = a_sb[e, h][:].rearrange("p (u v) s -> p v s u", u=2)
-            nc.scalar.activation(silu_neg[e, h][:], src, ACT.Silu, scale=-1.0)
-            nc.scalar.activation(neg_tanh[e, h][:], src, ACT.Tanh, scale=-0.5)
+            nc.scalar.activation(silu_sb[e, h][:], src, ACT.Silu, scale=-1.0)
+            nc.scalar.activation(tanh_sb[e, h][:], src, ACT.Tanh, scale=-0.5)
 
         def matmul_w2(e, h):
             for v in range(2):
-                slot = ((e * H_PASSES + h) * 2 + v) % 6
-                banks[e, h, v] = psum.tile([P, 2, C], F32, name=f"dh_bank{slot}")
+                turn = ((e * H_PASSES + h) * 2 + v) % DH_BANKS
+                dh_bank[e, h, v] = psum.tile([P, 2, C], F32, name=f"dh_bank{turn}")
                 for u in range(2):
                     col = (h * PACK + 2 * u + v) * P
                     nc.tensor.matmul_mx(
-                        out=banks[e, h, v][:, u, :],
+                        out=dh_bank[e, h, v][:, u, :],
                         lhsT=w2_perm[e][:, 2 * col : 2 * (col + P)].bitcast(FP4X4),
-                        lhsT_scale=s2_sb[e // GROUP][:, e % GROUP, col : col + P],
+                        lhsT_scale=s2_sb[e // TRIO][:, e % TRIO, col : col + P],
                         rhs=g_codes[e][:].bitcast(FP8X4),
                         rhs_scale=g_scales[e][:],
                         start=True,
                         stop=True,
                     )
 
-        def times_sigmoid(e, h, v):
+        def times_tanh(e, h, v):
             if v == 0:
-                x_sb[e, h] = ring.tile([P, 2, C, 2], F32, name="x_sb", bufs=3)
+                half_da[e, h] = ring.tile([P, 2, C, 2], F32, name="half_da", bufs=3)
             nc.vector.scalar_tensor_tensor(
-                x_sb[e, h][:, v],
-                neg_tanh[e, h][:, v],
+                half_da[e, h][:, v],
+                tanh_sb[e, h][:, v],
                 1.0,
-                banks[e, h, v][:].rearrange("p u s -> p s u"),
+                dh_bank[e, h, v][:].rearrange("p u s -> p s u"),
                 ALU.subtract,
                 ALU.mult,
             )
 
-        def finish_da(e, h):
+        def times_silu(e, h):
             if h == 0:
                 da_bf[e] = ring.tile([P, H_PASSES, C * PACK], BF16, name="da_bf", bufs=2, align_bytes=64)
             nc.vector.scalar_tensor_tensor(
                 da_bf[e][:, h, :].rearrange("p (y v) -> p y v", v=2),
-                silu_neg[e, h][:].rearrange("p v s u -> p (s u) v"),
+                silu_sb[e, h][:].rearrange("p v s u -> p (s u) v"),
                 1.0,
-                x_sb[e, h][:].rearrange("p v s u -> p (s u) v"),
+                half_da[e, h][:].rearrange("p v s u -> p (s u) v"),
                 ALU.subtract,
                 ALU.mult,
             )
@@ -205,16 +221,15 @@ def tile_moe_bdx_mlp_silu_kernel(
                 in_=da_bf[e][:, lo:hi, :].rearrange("p h x -> p (h x)"),
             )
 
+
         def matmul_w1(e):
-            if e % 2 == 0:
-                for b in range(K_BLOCKS):
-                    dx_bank[b] = psum.tile([P, 2 * C], F32, name=f"dx_bank{b}")
+            for b in range(K_BLOCKS):
+                dx_bank[b] = psum.tile([P, C], F32, name=f"dx_bank{b}")
             for h in range(H_PASSES):
                 for b in range(K_BLOCKS):
-                    row = (e % GROUP) * H_PASSES + h
                     nc.tensor.matmul_mx(
-                        out=dx_bank[b][:, (e % 2) * C : (e % 2 + 1) * C],
-                        lhsT=w1_sb[e // GROUP][:, row, 2 * b * P : 2 * (b + 1) * P].bitcast(FP4X4),
+                        out=dx_bank[b][:],
+                        lhsT=w1_sb[e // TRIO][:, (e % TRIO) * H_PASSES + h, 2 * b * P : 2 * (b + 1) * P].bitcast(FP4X4),
                         lhsT_scale=s1_sb[:, e * H_PASSES + h, b * P : (b + 1) * P],
                         rhs=da_codes[e][:, h * C : (h + 1) * C].bitcast(FP8X4),
                         rhs_scale=da_scales[e][:, h * C : (h + 1) * C],
@@ -222,140 +237,137 @@ def tile_moe_bdx_mlp_silu_kernel(
                         stop=(h == H_PASSES - 1),
                     )
 
-        def store_dx(e):
-            if e % 2 == 1:
-                for b in range(K_BLOCKS):
-                    nc.scalar.activation(dx_sb[b][:, (e - 1) * C : (e + 1) * C], dx_bank[b][:], ACT.Copy, scale=0.5)
-            elif e == E - 1:
-                nc.scalar.activation(dx_sb[1][:, e * C :], dx_bank[1][:, 0:C], ACT.Copy, scale=0.5)
-                nc.vector.tensor_scalar_mul(dx_sb[0][:, e * C :], dx_bank[0][:, 0:C], 0.5)
+        def copy_dx(e):
+            for b in range(K_BLOCKS):
+                dst = dx_sb[b][:, e * C : (e + 1) * C]
+                if b == 0 and (e < VECTOR_DX_EXPERTS or e == E - 1):
+                    nc.vector.tensor_scalar_mul(dst, dx_bank[b][:], 0.5)
+                else:
+                    nc.scalar.activation(dst, dx_bank[b][:], ACT.Copy, scale=0.5)
+
 
         load_s1()
         nc.sync.dma_start(offs_sb[:], offs)
-        load_a(0, [0])
+        load_a(0, 0)
         load_w2(0)
         load_gate(0)
-        nc.sync.dma_start(dy_sb[0][:], dy_rows[0])
-        nc.sync.dma_start(dy_sb[1][:], dy_rows[1])
-        nc.sync.dma_start(dy_sb[2][:], dy_rows[2])
-        nc.sync.dma_start(dy_sb[3][:], dy_rows[3])
+        for t in range(PACK):
+            nc.sync.dma_start(dy_sb[t][:], dy_rows[t])
         load_s2()
-        load_a(0, [1])
+        load_a(0, 1)
         load_gate(1)
         load_w2(1)
-        load_a(1)
+        load_a(1, 0)
+        load_a(1, 1)
         load_w2(2)
         load_w1(0)
-        load_a(2)
+        load_a(2, 0)
+        load_a(2, 1)
+
 
         activations(0, 0)
         gather_g(0)
-        gate_g(0)
+        new_g_bf(0)
+        gate_on_vector(0, 0)
         permute_w2(0)
         quantize_g(0)
         permute_s2(0, 1)
         gather_g(1)
         activations(0, 1)
         permute_w2(1)
-        permute_s2(1, GROUP)
-        gate_g(1)
+        permute_s2(1, TRIO)
+        new_g_bf(1)
+        gate_on_vector(1, 0)
         quantize_g(1)
+        gather_g(2)
+
+
+        last = E - 1
         for e in range(E):
-            if e == 0:
-                load_gate(2)
-                load_w2(3)
-                load_a(3)
-                move_s2(1)
-            if e == 1:
-                load_w2(4)
-                load_a(4)
-                load_w1(1)
-            if e == 2:
-                load_w2(5)
-                load_gate(3)
-                load_a(5)
-            if e == 3:
-                load_w2(6)
-                load_a(6)
-                move_s2(2)
-            if e == 4:
-                load_w2(7)
-                load_a(7)
-                load_w1(2)
-            if e == 5:
-                load_w2(8)
-                load_a(8)
-            if e == 6:
-                for lst, src in zip(pos_sb, (pos1, pos2, pos3)): nc.sync.dma_start(lst[:], src)
+            trio = e // TRIO + 1
+            if e % TRIO == 0 and trio < E // TRIO:
+                load_gate(trio + 1)
+            if e + LOAD_AHEAD <= last:
+                load_w2(e + LOAD_AHEAD)
+                load_a(e + LOAD_AHEAD, 0)
+                load_a(e + LOAD_AHEAD, 1)
+            if e % TRIO == 0 and trio < E // TRIO:
+                move_s2(trio)
+            if e % TRIO == 1 and trio < E // TRIO:
+                load_w1(trio)
+            if e + LOAD_AHEAD == E:
+                for lst, src in zip(pos_sb, (pos1, pos2, pos3)):
+                    nc.sync.dma_start(lst[:], src)
+
+            if e + 2 <= last:
+                new_g_bf(e + 2)
+                gate_on_gpsimd(e + 2)
             matmul_w2(e, 0)
             matmul_w2(e, 1)
-            if e + 1 < E:
-                activations(e + 1, 0)
-            times_sigmoid(e, 0, 0)
-            times_sigmoid(e, 0, 1)
-            times_sigmoid(e, 1, 0)
-            finish_da(e, 0)
             if e > 0:
                 matmul_w1(e - 1)
-                store_dx(e - 1)
-            times_sigmoid(e, 1, 1)
-            if e == E - 1:
-                quantize_da(e, 0, 1)
-            if e + 1 < E:
+            if e + 1 <= last:
+                activations(e + 1, 0)
+            if e + 3 <= last:
+                gather_g(e + 3)
+            for h in range(H_PASSES):
+                for v in range(2):
+                    times_tanh(e, h, v)
+            if e > 0:
+                copy_dx(e - 1)
+            if e + 1 <= last:
                 activations(e + 1, 1)
-            if e + 2 < E:
-                gather_g(e + 2)
+            times_silu(e, 0)
+            if e + 2 <= last:
+                gate_on_vector(e + 2, GPSIMD_SLOTS)
+            times_silu(e, 1)
+            if e + 2 <= last:
                 permute_w2(e + 2)
-            finish_da(e, 1)
-            if e + 2 < E:
-                gate_g(e + 2)
-            quantize_da(e, 1 if e == E - 1 else 0, H_PASSES)
-            if e + 2 < E:
+            if e < last:
+                quantize_da(e, 0, H_PASSES)
+            else:
+                quantize_da(e, 0, 1)
+                quantize_da(e, 1, H_PASSES)
+            if e + 2 <= last:
                 quantize_g(e + 2)
-        matmul_w1(E - 1)
-        store_dx(E - 1)
+        matmul_w1(last)
+        copy_dx(last)
 
-        def window(b, c, r):
-            lo, hi = TOKEN_CUTS[c], TOKEN_CUTS[c + 1]
-            return dx_sb[b][:].indirect(pos_sb[r][:, lo // LIST_ROWS : hi // LIST_ROWS])
+
+        cuts = (0, VECTOR_TOKENS, T)
+
+        def window_of(b, c, r):
+            return dx_sb[b][:].indirect(pos_sb[r][:, cuts[c] // LIST_ROWS : cuts[c + 1] // LIST_ROWS])
 
         def part(name, c):
-            return keep.tile([P, TOKEN_CUTS[c + 1] - TOKEN_CUTS[c]], F32, name=name)
+            return keep.tile([P, cuts[c + 1] - cuts[c]], F32, name=name)
 
-        def on_scalar(b, c, r):
+        def pick_on_scalar(b, c, r):
             picked = part(f"picked{b}{c}{r}", c)
-            nc.scalar.activation(picked[:], window(b, c, r), ACT.Copy)
+            nc.scalar.activation(picked[:], window_of(b, c, r), ACT.Copy)
             return picked
 
-        def on_vector(b, c, r):
+        def pick_on_vector(b, c, r):
             picked = part(f"picked{b}{c}{r}", c)
-            nc.vector.tensor_copy(picked[:], window(b, c, r))
+            nc.vector.tensor_copy(picked[:], window_of(b, c, r))
             return picked
 
-        def gather_add(b, c, r, other):
+        def pick_and_add(b, c, r, other):
             total = part(f"sum{b}{c}{r}", c)
-            nc.vector.tensor_tensor(total[:], window(b, c, r), other[:], ALU.add)
-            return total
-
-        def plain_add(b, c, x, y):
-            total = part(f"total{b}{c}", c)
-            nc.vector.tensor_tensor(total[:], x[:], y[:], ALU.add)
+            nc.vector.tensor_tensor(total[:], window_of(b, c, r), other[:], ALU.add)
             return total
 
         def store(b, c, total):
-            nc.sync.dma_start(out[b * P : (b + 1) * P, TOKEN_CUTS[c] : TOKEN_CUTS[c + 1]], total[:])
+            nc.sync.dma_start(out[b * P : (b + 1) * P, cuts[c] : cuts[c + 1]], total[:])
 
-        a11 = on_scalar(1, 1, 0)
-        a01 = on_scalar(0, 1, 0)
-        b11 = on_scalar(1, 1, 1)
-        b01 = on_scalar(0, 1, 1)
-        v00 = on_vector(0, 0, 0)
-        v10 = on_vector(1, 0, 0)
-        v00 = gather_add(0, 0, 1, v00)
-        v10 = gather_add(1, 0, 1, v10)
-        store(0, 0, gather_add(0, 0, 2, v00))
-        store(1, 0, gather_add(1, 0, 2, v10))
-        v11 = gather_add(1, 1, 2, a11)
-        v01 = gather_add(0, 1, 2, a01)
-        store(1, 1, plain_add(1, 1, v11, b11))
-        store(0, 1, plain_add(0, 1, v01, b01))
+        blocks = range(K_BLOCKS)
+        wide = {(b, r): pick_on_scalar(b, 1, r) for r in range(2) for b in reversed(blocks)}
+        narrow = [pick_on_vector(b, 0, 0) for b in blocks]
+        narrow = [pick_and_add(b, 0, 1, narrow[b]) for b in blocks]
+        for b in blocks:
+            store(b, 0, pick_and_add(b, 0, 2, narrow[b]))
+        two_of_three = {b: pick_and_add(b, 1, 2, wide[b, 0]) for b in reversed(blocks)}
+        for b in reversed(blocks):
+            total = part(f"total{b}", 1)
+            nc.vector.tensor_tensor(total[:], two_of_three[b][:], wide[b, 1][:], ALU.add)
+            store(b, 1, total)

from contextlib import ExitStack

import concourse.mybir as mybir

K, T, E, C, H, N = 256, 768, 9, 256, 1024, 512
S = E * C
P = 128
PACK = 4
H_PASSES = H // (P * PACK)
K_BLOCKS = K // P
LIST_ROWS = 16
SCALE_ROWS = 16
QUADRANT = 32
TRIO = 3

FLOPS = 2 * S * (N * H + H * K)

F32 = mybir.dt.float32
BF16 = mybir.dt.bfloat16
I32 = mybir.dt.int32
U32 = mybir.dt.uint32
U16 = mybir.dt.uint16
U8 = mybir.dt.uint8
FP8X4 = mybir.dt.float8_e4m3fn_x4
FP4X4 = mybir.dt.float4_e2m1fn_x4
ACT = mybir.ActivationFunctionType
ALU = mybir.AluOpType

GATE_LOADS = ((0, 1), (1, TRIO), (TRIO, 2 * TRIO), (2 * TRIO, E))
PARKED = {1: 4, 2: 72}
DH_BANKS = 6
LOAD_AHEAD = 3

GPSIMD_SLOTS = 160
VECTOR_DX_EXPERTS = 4
VECTOR_TOKENS = 160


def tile_moe_bdx_mlp_silu_kernel(
    tc, dyT, a, w2_words, w2_scales, w1_words, w1_scales, gate, offs, pos1, pos2, pos3, out
):
    nc = tc.nc
    with ExitStack() as ctx:
        keep = ctx.enter_context(tc.tile_pool(name="keep", bufs=1))
        ring = ctx.enter_context(tc.tile_pool(name="ring", bufs=2))
        psum = ctx.enter_context(tc.psum_pool(name="psum", bufs=1))

        offs_sb = keep.tile([P, S // LIST_ROWS], U16, name="offs_sb")
        pos_sb = [keep.tile([P, T // LIST_ROWS], U16, name=f"pos_sb{r}") for r in range(3)]
        dy_sb = [keep.tile([P, T], F32, name=f"dy_sb{t}") for t in range(PACK)]
        gate_sb = [keep.tile([P, (hi - lo) * C], F32, name=f"gate_sb{lo}") for lo, hi in GATE_LOADS]
        w1_sb = [
            keep.tile([P, TRIO * H_PASSES, 2 * K], U8, name=f"w1_sb{j}", align_bytes=64) for j in range(E // TRIO)
        ]
        s1_sb = keep.tile([P, E * H_PASSES, K], U8, name="s1_sb", align_bytes=64)
        s2_raw = keep.tile([P, TRIO, H], U8, name="s2_raw", align_bytes=64)
        s2_sb = [keep.tile([P, TRIO, H], U8, name=f"s2_sb{j}", align_bytes=64) for j in range(E // TRIO)]
        dx_sb = [keep.tile([P, S], F32, name=f"dx_sb{b}") for b in range(K_BLOCKS)]

        nc.vector.memset(s2_raw[:].rearrange("p e i -> p (e i)").bitcast(I32), 0)
        nc.gpsimd.memset(s1_sb[:].rearrange("p e k -> p (e k)").bitcast(I32), 0)
        for plane in s2_sb[1:]:
            nc.vector.memset(plane[:].rearrange("p e i -> p (e i)").bitcast(I32), 0)

        a_sb, w2_raw, w2_perm = {}, {}, {}
        g_f32, g_bf, g_codes, g_scales = {}, {}, {}, {}
        tanh_sb, silu_sb, dh_bank, half_da = {}, {}, {}, {}
        da_bf, da_codes, da_scales, dx_bank = {}, {}, {}, {}

        dy_rows = dyT.rearrange("(p t) c -> t p c", t=PACK)
        a_rows = a.rearrange("(h p t) j -> h p t j", h=H_PASSES, t=PACK)


        def load_a(e, h):
            a_sb[e, h] = ring.tile([P, PACK, C], F32, name="a_sb", bufs=8)
            nc.sync.dma_start(a_sb[e, h][:], a_rows[h][:, :, e * C : (e + 1) * C])

        def load_w2(e):
            w2_raw[e] = ring.tile([P, 2 * H], U8, name="w2_raw", bufs=4, align_bytes=64)
            nc.sync.dma_start(w2_raw[e][:].bitcast(I32), w2_words[e, 0].bitcast(I32))

        def load_gate(j):
            lo, hi = GATE_LOADS[j]
            nc.sync.dma_start(gate_sb[j][:], gate[0:P, lo * C : hi * C])

        def load_w1(j):
            src = w1_words[j * TRIO : (j + 1) * TRIO].rearrange("e s p b -> p (e s) b")
            nc.sync.dma_start(w1_sb[j][:].bitcast(I32), src.bitcast(I32))

        def load_s1():
            src = w1_scales.rearrange("e s (q r) k -> r q (e s) k", r=4)
            for r in range(4):
                nc.gpsimd.dma_start(s1_sb[r:P:QUADRANT].bitcast(I32), src[r].bitcast(I32))

        def load_s2():
            src = w2_scales[0:TRIO].rearrange("e s (q r) i -> r q (e s) i", r=4)
            for r in range(4):
                nc.sync.dma_start(s2_raw[r:P:QUADRANT].bitcast(I32), src[r].bitcast(I32))
            for j, first in PARKED.items():
                rows = w2_scales[j * TRIO : (j + 1) * TRIO].rearrange("e s f i -> f (e s) i")
                nc.sync.dma_start(s2_raw[first : first + SCALE_ROWS].bitcast(I32), rows.bitcast(I32))

        def move_s2(j):
            for q in range(4):
                first = PARKED[j] + 4 * q
                nc.sync.dma_start(
                    s2_sb[j][QUADRANT * q : QUADRANT * q + 4].bitcast(I32), s2_sb[0][first : first + 4].bitcast(I32)
                )


        def permute_w2(e):
            copy = nc.scalar.copy if e == E - 1 else nc.vector.tensor_copy
            w2_perm[e] = ring.tile([P, 2 * H], U8, name="w2_perm", bufs=3, align_bytes=64)
            copy(
                w2_perm[e][:].bitcast(U16).rearrange("p (h t m) -> p h t m", h=H_PASSES, t=PACK),
                w2_raw[e][:].bitcast(U16).rearrange("p (h m t) -> p h t m", h=H_PASSES, t=PACK),
            )

        def permute_s2(lo, hi):
            nc.vector.tensor_copy(
                s2_sb[0][:, lo:hi, :].rearrange("p e (h t m) -> p (e h) t m", h=H_PASSES, t=PACK),
                s2_raw[:, lo:hi, :].rearrange("p e (h m t) -> p (e h) t m", h=H_PASSES, t=PACK),
            )


        def gates_of(e):
            j = [lo <= e < hi for lo, hi in GATE_LOADS].index(True)
            first = (e - GATE_LOADS[j][0]) * C
            return gate_sb[j][:, first : first + C]

        def gather_g(e):
            g_f32[e] = ring.tile([P, PACK, C], F32, name="g_f32", bufs=3)
            cols = slice(e * C // LIST_ROWS, (e + 1) * C // LIST_ROWS)
            for t in range(PACK):
                window = dy_sb[t][:].indirect(offs_sb[:, cols])
                if e == 0:
                    nc.vector.tensor_tensor(g_f32[e][:, t, :], window, gates_of(e), ALU.mult)
                else:
                    nc.scalar.activation(g_f32[e][:, t, :], window, ACT.Copy)

        def new_g_bf(e):
            g_bf[e] = ring.tile([P, C * PACK], BF16, name="g_bf", bufs=1, align_bytes=64)

        def gate_on_gpsimd(e):
            nc.gpsimd.tensor_tensor(
                g_bf[e][:, : GPSIMD_SLOTS * PACK].rearrange("p (s t) -> p s t", t=PACK),
                g_f32[e][:, :, :GPSIMD_SLOTS].rearrange("p t s -> p s t"),
                gates_of(e)[:, :GPSIMD_SLOTS].unsqueeze(2).to_broadcast([P, GPSIMD_SLOTS, PACK]),
                ALU.mult,
            )

        def gate_on_vector(e, first):
            dst = g_bf[e][:, first * PACK :].rearrange("p (c i t) -> p c t i", i=2, t=PACK)
            src = g_f32[e][:, :, first:].rearrange("p t (c i) -> p c t i", i=2)
            if e == 0:
                nc.vector.tensor_copy(dst, src)
            else:
                gates = gates_of(e)[:, first:].rearrange("p (c i) -> p c i", i=2).unsqueeze(2)
                nc.vector.tensor_tensor(dst, src, gates.to_broadcast([P, (C - first) // 2, PACK, 2]), ALU.mult)

        def quantize_g(e):
            g_codes[e] = ring.tile([P, C], U32, name="g_codes", bufs=3, align_bytes=64)
            g_scales[e] = ring.tile([P, C], U8, name="g_scales", bufs=3, align_bytes=64)
            nc.vector.quantize_mx(out=g_codes[e][:].bitcast(FP8X4), scales=g_scales[e][:], in_=g_bf[e][:])


        def activations(e, h):
            tanh_sb[e, h] = ring.tile([P, 2, C, 2], F32, name="tanh_sb", bufs=4)
            silu_sb[e, h] = ring.tile([P, 2, C, 2], F32, name="silu_sb", bufs=4)
            src = a_sb[e, h][:].rearrange("p (u v) s -> p v s u", u=2)
            nc.scalar.activation(silu_sb[e, h][:], src, ACT.Silu, scale=-1.0)
            nc.scalar.activation(tanh_sb[e, h][:], src, ACT.Tanh, scale=-0.5)

        def matmul_w2(e, h):
            for v in range(2):
                turn = ((e * H_PASSES + h) * 2 + v) % DH_BANKS
                dh_bank[e, h, v] = psum.tile([P, 2, C], F32, name=f"dh_bank{turn}")
                for u in range(2):
                    col = (h * PACK + 2 * u + v) * P
                    nc.tensor.matmul_mx(
                        out=dh_bank[e, h, v][:, u, :],
                        lhsT=w2_perm[e][:, 2 * col : 2 * (col + P)].bitcast(FP4X4),
                        lhsT_scale=s2_sb[e // TRIO][:, e % TRIO, col : col + P],
                        rhs=g_codes[e][:].bitcast(FP8X4),
                        rhs_scale=g_scales[e][:],
                        start=True,
                        stop=True,
                    )

        def times_tanh(e, h, v):
            if v == 0:
                half_da[e, h] = ring.tile([P, 2, C, 2], F32, name="half_da", bufs=3)
            nc.vector.scalar_tensor_tensor(
                half_da[e, h][:, v],
                tanh_sb[e, h][:, v],
                1.0,
                dh_bank[e, h, v][:].rearrange("p u s -> p s u"),
                ALU.subtract,
                ALU.mult,
            )

        def times_silu(e, h):
            if h == 0:
                da_bf[e] = ring.tile([P, H_PASSES, C * PACK], BF16, name="da_bf", bufs=2, align_bytes=64)
            nc.vector.scalar_tensor_tensor(
                da_bf[e][:, h, :].rearrange("p (y v) -> p y v", v=2),
                silu_sb[e, h][:].rearrange("p v s u -> p (s u) v"),
                1.0,
                half_da[e, h][:].rearrange("p v s u -> p (s u) v"),
                ALU.subtract,
                ALU.mult,
            )

        def quantize_da(e, lo, hi):
            if lo == 0:
                da_codes[e] = ring.tile([P, H_PASSES * C], U32, name="da_codes", bufs=2, align_bytes=64)
                da_scales[e] = ring.tile([P, H_PASSES * C], U8, name="da_scales", bufs=2, align_bytes=64)
            nc.vector.quantize_mx(
                out=da_codes[e][:, lo * C : hi * C].bitcast(FP8X4),
                scales=da_scales[e][:, lo * C : hi * C],
                in_=da_bf[e][:, lo:hi, :].rearrange("p h x -> p (h x)"),
            )


        def matmul_w1(e):
            for b in range(K_BLOCKS):
                dx_bank[b] = psum.tile([P, C], F32, name=f"dx_bank{b}")
            for h in range(H_PASSES):
                for b in range(K_BLOCKS):
                    nc.tensor.matmul_mx(
                        out=dx_bank[b][:],
                        lhsT=w1_sb[e // TRIO][:, (e % TRIO) * H_PASSES + h, 2 * b * P : 2 * (b + 1) * P].bitcast(FP4X4),
                        lhsT_scale=s1_sb[:, e * H_PASSES + h, b * P : (b + 1) * P],
                        rhs=da_codes[e][:, h * C : (h + 1) * C].bitcast(FP8X4),
                        rhs_scale=da_scales[e][:, h * C : (h + 1) * C],
                        start=(h == 0),
                        stop=(h == H_PASSES - 1),
                    )

        def copy_dx(e):
            for b in range(K_BLOCKS):
                dst = dx_sb[b][:, e * C : (e + 1) * C]
                if b == 0 and (e < VECTOR_DX_EXPERTS or e == E - 1):
                    nc.vector.tensor_scalar_mul(dst, dx_bank[b][:], 0.5)
                else:
                    nc.scalar.activation(dst, dx_bank[b][:], ACT.Copy, scale=0.5)


        load_s1()
        nc.sync.dma_start(offs_sb[:], offs)
        load_a(0, 0)
        load_w2(0)
        load_gate(0)
        for t in range(PACK):
            nc.sync.dma_start(dy_sb[t][:], dy_rows[t])
        load_s2()
        load_a(0, 1)
        load_gate(1)
        load_w2(1)
        load_a(1, 0)
        load_a(1, 1)
        load_w2(2)
        load_w1(0)
        load_a(2, 0)
        load_a(2, 1)


        activations(0, 0)
        gather_g(0)
        new_g_bf(0)
        gate_on_vector(0, 0)
        permute_w2(0)
        quantize_g(0)
        permute_s2(0, 1)
        gather_g(1)
        activations(0, 1)
        permute_w2(1)
        permute_s2(1, TRIO)
        new_g_bf(1)
        gate_on_vector(1, 0)
        quantize_g(1)
        gather_g(2)


        last = E - 1
        for e in range(E):
            trio = e // TRIO + 1
            if e % TRIO == 0 and trio < E // TRIO:
                load_gate(trio + 1)
            if e + LOAD_AHEAD <= last:
                load_w2(e + LOAD_AHEAD)
                load_a(e + LOAD_AHEAD, 0)
                load_a(e + LOAD_AHEAD, 1)
            if e % TRIO == 0 and trio < E // TRIO:
                move_s2(trio)
            if e % TRIO == 1 and trio < E // TRIO:
                load_w1(trio)
            if e + LOAD_AHEAD == E:
                for lst, src in zip(pos_sb, (pos1, pos2, pos3)):
                    nc.sync.dma_start(lst[:], src)

            if e + 2 <= last:
                new_g_bf(e + 2)
                gate_on_gpsimd(e + 2)
            matmul_w2(e, 0)
            matmul_w2(e, 1)
            if e > 0:
                matmul_w1(e - 1)
            if e + 1 <= last:
                activations(e + 1, 0)
            if e + 3 <= last:
                gather_g(e + 3)
            for h in range(H_PASSES):
                for v in range(2):
                    times_tanh(e, h, v)
            if e > 0:
                copy_dx(e - 1)
            if e + 1 <= last:
                activations(e + 1, 1)
            times_silu(e, 0)
            if e + 2 <= last:
                gate_on_vector(e + 2, GPSIMD_SLOTS)
            times_silu(e, 1)
            if e + 2 <= last:
                permute_w2(e + 2)
            if e < last:
                quantize_da(e, 0, H_PASSES)
            else:
                quantize_da(e, 0, 1)
                quantize_da(e, 1, H_PASSES)
            if e + 2 <= last:
                quantize_g(e + 2)
        matmul_w1(last)
        copy_dx(last)


        cuts = (0, VECTOR_TOKENS, T)

        def window_of(b, c, r):
            return dx_sb[b][:].indirect(pos_sb[r][:, cuts[c] // LIST_ROWS : cuts[c + 1] // LIST_ROWS])

        def part(name, c):
            return keep.tile([P, cuts[c + 1] - cuts[c]], F32, name=name)

        def pick_on_scalar(b, c, r):
            picked = part(f"picked{b}{c}{r}", c)
            nc.scalar.activation(picked[:], window_of(b, c, r), ACT.Copy)
            return picked

        def pick_on_vector(b, c, r):
            picked = part(f"picked{b}{c}{r}", c)
            nc.vector.tensor_copy(picked[:], window_of(b, c, r))
            return picked

        def pick_and_add(b, c, r, other):
            total = part(f"sum{b}{c}{r}", c)
            nc.vector.tensor_tensor(total[:], window_of(b, c, r), other[:], ALU.add)
            return total

        def store(b, c, total):
            nc.sync.dma_start(out[b * P : (b + 1) * P, cuts[c] : cuts[c + 1]], total[:])

        blocks = range(K_BLOCKS)
        wide = {(b, r): pick_on_scalar(b, 1, r) for r in range(2) for b in reversed(blocks)}
        narrow = [pick_on_vector(b, 0, 0) for b in blocks]
        narrow = [pick_and_add(b, 0, 1, narrow[b]) for b in blocks]
        for b in blocks:
            store(b, 0, pick_and_add(b, 0, 2, narrow[b]))
        two_of_three = {b: pick_and_add(b, 1, 2, wide[b, 0]) for b in reversed(blocks)}
        for b in reversed(blocks):
            total = part(f"total{b}", 1)
            nc.vector.tensor_tensor(total[:], two_of_three[b][:], wide[b, 1][:], ALU.add)
            store(b, 1, total)
